import numpy as np
import ml_dtypes


def mxq(x, axis, fmt="e4m3"):
    dtype, down = {"e4m3": (ml_dtypes.float8_e4m3fn, 7), "e5m2": (ml_dtypes.float8_e5m2, 14)}[fmt]
    v = np.moveaxis(np.asarray(x, np.float32).astype(ml_dtypes.bfloat16).astype(np.float64), axis, -1)
    blocks = v.reshape(v.shape[:-1] + (-1, 32))
    amax = np.abs(blocks).max(-1, keepdims=True)
    byte = np.maximum(np.where(amax > 0, np.frexp(amax)[1] - 1 + 127, 0) - down, 1)
    scale = np.exp2(byte - 127.0)
    codes = (blocks / scale).astype(np.float32).astype(dtype).astype(np.float64)
    return np.moveaxis((codes * scale).reshape(v.shape), -1, axis)


WIDE = False


def mx_kscale(k):
    if not WIDE:
        return np.ones(k)
    levels = np.array([10, -10, 5, -5, 0])
    if k % 512:
        return np.exp2(np.random.permutation(np.resize(levels, k // 32))).repeat(32)
    a = np.empty((k // 512, 16))
    for p in range(k // 512):
        a[p, :8] = np.random.permutation(np.resize(levels, 8))
        for g in range(8):
            far = levels[np.abs(levels - a[p, g]) >= 10]
            a[p, g + 8] = far[np.random.randint(len(far))]
    return np.exp2(a.ravel()).repeat(32)


def f64(x):
    return np.asarray(x).astype(np.float64)


def striped8(idx):
    return np.asarray(idx).reshape(8, -1, 16).transpose(0, 2, 1).reshape(128, -1).astype(np.uint16)


def unstriped8(offs):
    return offs.reshape(8, 16, -1).transpose(0, 2, 1).reshape(8, -1).astype(np.int64)


def pick8(x, idx, run):
    r = np.arange(len(x))
    return x[r[:, None], idx[r % (8 * run) // run]]


E2M1 = np.array([0.0, 0.5, 1.0, 1.5, 2.0, 3.0, 4.0, 6.0, -0.0, -0.5, -1.0, -1.5, -2.0, -3.0, -4.0, -6.0])


def pack_weight(w, fmt):
    k, n = w.shape
    w = f64(np.asarray(w, np.float32).astype(ml_dtypes.bfloat16)).reshape(k // 32, 32, n)
    amax = np.abs(w).max(1)
    if fmt == "e4m3":
        byte = np.frexp(amax)[1] - 1 + 127 - 7
    else:
        mant, ex = np.frexp(amax / 6.0)
        byte = np.where(mant > 0.5, ex, ex - 1) + 127
    byte = np.clip(np.where(amax > 0, byte, 1), 1, 254)
    scaled = (w * np.exp2(127.0 - byte)[:, None, :]).reshape(k, n).astype(np.float32)
    by_word = np.ascontiguousarray(scaled.reshape(k // 512, 128, 4, n).transpose(0, 1, 3, 2))
    if fmt == "e4m3":
        words = by_word.astype(ml_dtypes.float8_e4m3fn).view(np.uint8)
    else:
        c = by_word.astype(ml_dtypes.float4_e2m1fn).view(np.uint8) & 0xF
        words = (c[..., 0::2] | (c[..., 1::2] << 4)).reshape(k // 512, 128, 2 * n)
    return np.ascontiguousarray(words), np.ascontiguousarray(byte.astype(np.uint8).reshape(k // 512, 16, n))


def unpack_weight(words, scales, fmt):
    g, _, n = scales.shape
    words = np.ascontiguousarray(words).reshape(g, 128, n, -1)
    if fmt == "e4m3":
        vals = words.view(ml_dtypes.float8_e4m3fn).astype(np.float64)
    else:
        nib = np.empty((g, 128, n, 4), np.uint8)
        nib[..., 0::2] = words & 0xF
        nib[..., 1::2] = words >> 4
        vals = E2M1[nib]
    vals = vals * np.repeat(np.exp2(scales.astype(np.float64) - 127.0), 8, axis=1)[..., None]
    return vals.transpose(0, 1, 3, 2).reshape(g * 512, n)


D, T, I, Q = 512, 1024, 512, 128


def setup_inputs():
    n = np.random.standard_normal
    idx = np.stack([np.random.permutation(T)[:I] for _ in range(8)])
    idx2 = np.stack([np.random.permutation(T)[:I] for _ in range(8)])
    idx3 = np.stack([np.random.permutation(T)[:I] for _ in range(8)])
    idx4 = np.stack([np.random.permutation(T)[:I] for _ in range(8)])
    fd = mx_kscale(D)
    keysp = pack_weight(n((D, T)) / fd[:, None], "e2m1")
    return {
        "query": (n((D, Q)) * 0.9 / np.sqrt(D) * fd[:, None]).astype(np.float32),
        "query2": (n((D, Q)) * 0.9 / np.sqrt(D) * fd[:, None]).astype(np.float32),
        "keys_words": keysp[0],
        "keys_scales": keysp[1],
        "lam": (np.random.uniform(1.0, 2.5, (Q, 1))).astype(np.float32),
        "old": (1.0 * n((Q, T))).astype(np.float32),
        "share2": (np.random.uniform(0.4, 1.2, (Q, 1))).astype(np.float32),
        "offs": striped8(idx),
        "offs2": striped8(idx2),
        "offs3": striped8(idx3),
        "offs4": striped8(idx4),
    }


def reference(query, query2, keys_words, keys_scales, lam, old, share2, offs, offs2, offs3, offs4):
    idx = unstriped8(offs)
    idx2 = unstriped8(offs2)
    idx3 = unstriped8(offs3)
    idx4 = unstriped8(offs4)
    keysu = unpack_weight(keys_words, keys_scales, "e2m1")
    queryq = mxq(f64(query), 0, "e4m3")
    a = queryq.T @ keysu
    query2q = mxq(f64(query2), 0, "e4m3")
    b = query2q.T @ keysu
    e1s = np.exp(pick8(a, idx, 16))
    w = e1s / (e1s + np.exp(pick8(a, idx2, 16)) + np.exp(pick8(b, idx3, 16))) * f64(lam)
    f1 = np.zeros((Q, T))
    f1[np.arange(Q)[:, None], idx[np.arange(Q) % 128 // 16]] = w
    f2 = np.zeros((Q, T))
    f2[np.arange(Q)[:, None], idx4[np.arange(Q) % 128 // 16]] = w
    y = f64(old) + f1 + f2 * f64(share2)
    return y

@@ -1,0 +1,184 @@
+from contextlib import ExitStack
+
+import concourse.mybir as mybir
+from concourse.masks import make_identity
+
+F32 = mybir.dt.float32
+BF16 = mybir.dt.bfloat16
+I32 = mybir.dt.int32
+U32 = mybir.dt.uint32
+U16 = mybir.dt.uint16
+U8 = mybir.dt.uint8
+FP8X4 = mybir.dt.float8_e4m3fn_x4
+FP4X4 = mybir.dt.float4_e2m1fn_x4
+ACT = mybir.ActivationFunctionType
+ALU = mybir.AluOpType
+
+P = 128
+D, T, SLOTS, Q = 512, 1024, 512, 128
+BANK = 512
+FLOPS = 2 * 2 * D * T * Q
+
+
+def tile_attend_quotaratio_lean_twiceput_heads_kernel(
+    tc, query, query2, keys_words, keys_scales, lam, old, share2, offs, offs2, offs3, offs4, out
+):
+    nc = tc.nc
+    with ExitStack() as ctx:
+        lists = ctx.enter_context(tc.tile_pool(name="lists", bufs=1))
+        sb = ctx.enter_context(tc.tile_pool(name="sb", bufs=1))
+        psum = ctx.enter_context(tc.psum_pool(name="psum", bufs=1))
+
+        def cols(lst, s0, s1):
+            return lst[:, s0 // 16 : s1 // 16]
+
+        key_scales = sb.tile([P, T], U8, name="key_scales", align_bytes=64)
+        nc.vector.memset(key_scales[:].bitcast(I32), 0)
+        q_raw = sb.tile([P, 4, Q], F32, name="q_raw")
+        nc.sync.dma_start(out=q_raw[:], in_=query.rearrange("(p j) q -> p j q", j=4))
+        for quad in range(4):
+            nc.scalar.dma_start(
+                out=key_scales[32 * quad : 32 * quad + 4, :].bitcast(I32),
+                in_=keys_scales[0, 4 * quad : 4 * quad + 4, :].bitcast(I32),
+            )
+        key_words = sb.tile([P, 2 * T], U8, name="key_words", align_bytes=64)
+        nc.sync.dma_start(out=key_words[:].bitcast(I32), in_=keys_words[0].bitcast(I32))
+        q2_raw = sb.tile([P, 4, Q], F32, name="q2_raw")
+        nc.sync.dma_start(out=q2_raw[:], in_=query2.rearrange("(p j) q -> p j q", j=4))
+        list1 = lists.tile([P, SLOTS // 16], U16, name="list1")
+        list2 = lists.tile([P, SLOTS // 16], U16, name="list2")
+        list3 = lists.tile([P, SLOTS // 16], U16, name="list3")
+        list4 = lists.tile([P, SLOTS // 16], U16, name="list4")
+        lam_sb = sb.tile([P, 1], F32, name="lam_sb")
+        share_sb = sb.tile([P, 1], F32, name="share_sb")
+        old_sb = sb.tile([P, T], F32, name="old_sb")
+        nc.sync.dma_start(list1[:], offs)
+        nc.sync.dma_start(out=lam_sb[:], in_=lam)
+        nc.sync.dma_start(list2[:], offs2)
+        nc.sync.dma_start(list3[:], offs3)
+        nc.sync.dma_start(out=old_sb[:], in_=old)
+        nc.sync.dma_start(list4[:], offs4)
+        nc.sync.dma_start(out=share_sb[:], in_=share2)
+
+        f1 = sb.tile([P, T], F32, name="f1")
+        f2 = sb.tile([P, T], F32, name="f2")
+        nc.vector.memset(f1[:], 0.0)
+        nc.vector.memset(f2[:], 0.0)
+        ident = sb.tile([P, P], F32, name="ident")
+        make_identity(nc, ident[:])
+
+        def quantise(raw, name):
+            grouped = sb.tile([P, Q, 4], BF16, name=name + "_bf", align_bytes=64)
+            nc.vector.tensor_copy(out=grouped[:], in_=raw[:].rearrange("p j q -> p q j"))
+            codes = sb.tile([P, Q], U32, name=name + "_codes", align_bytes=64)
+            scales = sb.tile([P, Q], U8, name=name + "_scales", align_bytes=64)
+            nc.vector.quantize_mx(
+                out=codes[:].bitcast(FP8X4), scales=scales[:], in_=grouped[:].rearrange("p q j -> p (q j)")
+            )
+            return codes, scales
+
+        def score(codes, scales, c0, width, tag):
+            bank = psum.tile([P, width], F32, name=tag, tag=tag)
+            nc.tensor.matmul_mx(
+                out=bank[:],
+                lhsT=codes[:].bitcast(FP8X4),
+                lhsT_scale=scales[:],
+                rhs=key_words[:, 2 * c0 : 2 * (c0 + width)].bitcast(FP4X4),
+                rhs_scale=key_scales[:, c0 : c0 + width],
+                start=True,
+                stop=True,
+            )
+            return bank
+
+        W = 256
+        qc, qs = quantise(q_raw, "q")
+        a_banks = [score(qc, qs, c * W, W, "bank%d" % c) for c in range(4)]
+        q2c, q2s = quantise(q2_raw, "q2")
+        b_banks = [score(q2c, q2s, h * BANK, BANK, "bank%d" % (4 + h)) for h in range(2)]
+
+        EARLY = 128
+        lam_wide = sb.tile([P, EARLY], F32, name="lam_wide")
+        nc.scalar.activation(out=lam_wide[:], in_=lam_sb[:].to_broadcast([P, EARLY]), func=ACT.Copy)
+
+        a_sb = sb.tile([P, T], F32, name="a_sb")
+        b_sb = sb.tile([P, T], F32, name="b_sb")
+        for c in range(3):
+            nc.scalar.copy(out=a_sb[:, c * W : (c + 1) * W], in_=a_banks[c][:])
+        nc.vector.tensor_copy(out=a_sb[:, 3 * W :], in_=a_banks[3][:])
+        nc.vector.tensor_copy(out=b_sb[:, :BANK], in_=b_banks[0][:])
+
+        H = SLOTS // 2
+        g1 = [sb.tile([P, H], F32, name="g1_%d" % h) for h in range(2)]
+        diff = [sb.tile([P, 2, H], F32, name="diff%d" % h) for h in range(2)]
+        ex = sb.tile([P, 2, SLOTS], F32, name="ex")
+        den = sb.tile([P, SLOTS], F32, name="den")
+        nc.scalar.activation(out=g1[0][:], in_=a_sb[:].indirect(cols(list1, 0, H)), func=ACT.Copy)
+        nc.scalar.copy(out=b_sb[:, BANK:], in_=b_banks[1][:])
+        nc.scalar.activation(out=g1[1][:], in_=a_sb[:].indirect(cols(list1, H, SLOTS)), func=ACT.Copy)
+        for h in range(2):
+            nc.vector.tensor_tensor(
+                out=diff[h][:, 0, :], in0=a_sb[:].indirect(cols(list2, h * H, (h + 1) * H)), in1=g1[h][:],
+                op=ALU.subtract,
+            )
+            nc.vector.tensor_tensor(
+                out=diff[h][:, 1, :], in0=b_sb[:].indirect(cols(list3, h * H, (h + 1) * H)), in1=g1[h][:],
+                op=ALU.subtract,
+            )
+            nc.scalar.activation(out=ex[:, :, h * H : (h + 1) * H], in_=diff[h][:], func=ACT.Exp)
+
+        def denominator(s0, s1):
+            nc.vector.scalar_tensor_tensor(
+                out=den[:, s0:s1], in0=ex[:, 0, s0:s1], scalar=1.0, in1=ex[:, 1, s0:s1], op0=ALU.add, op1=ALU.add
+            )
+
+        denominator(0, EARLY)
+        inv = sb.tile([P, EARLY], F32, name="inv")
+        nc.vector.reciprocal(out=inv[:], in_=den[:, :EARLY])
+        denominator(EARLY, SLOTS)
+        nc.vector.tensor_tensor(out=f1[:].indirect(cols(list1, 0, EARLY)), in0=inv[:], in1=lam_wide[:], op=ALU.mult)
+        nc.vector.tensor_tensor(out=f2[:].indirect(cols(list4, 0, EARLY)), in0=inv[:], in1=lam_wide[:], op=ALU.mult)
+
+        turn_banks = [psum.tile([P, W], F32, name="turn%d" % c, tag="bank%d" % c) for c in range(4)]
+        for c in range(4):
+            for j in range(2):
+                c0 = c * W + j * P
+                nc.tensor.matmul(
+                    turn_banks[c][:, j * P : (j + 1) * P], lhsT=old_sb[:, c0 : c0 + P], rhs=ident[:],
+                    is_transpose=True, start=(j == 0), stop=False,
+                )
+
+        pieces = [(EARLY, H), (H, SLOTS)]
+        root = sb.tile([P, SLOTS], F32, name="root")
+        root_lam = sb.tile([P, SLOTS], F32, name="root_lam")
+        for s0, s1 in pieces:
+            nc.scalar.activation(out=root[:, s0:s1], in_=den[:, s0:s1], func=ACT.Abs_reciprocal_sqrt)
+        for s0, s1 in pieces:
+            nc.scalar.activation(out=root_lam[:, s0:s1], in_=root[:, s0:s1], func=ACT.Copy, scale=lam_sb[:])
+        nc.vector.tensor_tensor(
+            out=f1[:].indirect(cols(list1, EARLY, SLOTS)), in0=root[:, EARLY:], in1=root_lam[:, EARLY:], op=ALU.mult
+        )
+        nc.vector.tensor_tensor(
+            out=f2[:].indirect(cols(list4, EARLY, SLOTS)), in0=root[:, EARLY:], in1=root_lam[:, EARLY:], op=ALU.mult
+        )
+
+        turned = [sb.tile([P, W], F32, name="turned%d" % c) for c in range(4)]
+        back_banks = [psum.tile([P, W], F32, name="back%d" % c, tag="bank%d" % (4 + c)) for c in range(4)]
+        for c in range(4):
+            for j in range(2):
+                c0 = c * W + j * P
+                nc.tensor.matmul(
+                    turn_banks[c][:, j * P : (j + 1) * P], lhsT=f1[:, c0 : c0 + P], rhs=ident[:],
+                    is_transpose=True, start=False, stop=(j == 1),
+                )
+            nc.scalar.copy(out=turned[c][:], in_=turn_banks[c][:])
+        for c in range(4):
+            for j in range(2):
+                nc.tensor.transpose(back_banks[c][:, j * P : (j + 1) * P], turned[c][:, j * P : (j + 1) * P], ident[:])
+
+        for c in range(T // W):
+            res = sb.tile([P, W], F32, name="res%d" % c)
+            nc.vector.scalar_tensor_tensor(
+                out=res[:], in0=f2[:, c * W : (c + 1) * W], scalar=share_sb[:], in1=back_banks[c][:],
+                op0=ALU.mult, op1=ALU.add,
+            )
+            nc.sync.dma_start(out=out[:, c * W : (c + 1) * W], in_=res[:])

@@ -33,18 +33,17 @@ def tile_attend_quotaratio_lean_twiceput_heads_kernel(
             return lst[:, s0 // 16 : s1 // 16]
 
         key_scales = sb.tile([P, T], U8, name="key_scales", align_bytes=64)
-        nc.vector.memset(key_scales[:].bitcast(I32), 0)
         q_raw = sb.tile([P, 4, Q], F32, name="q_raw")
         nc.sync.dma_start(out=q_raw[:], in_=query.rearrange("(p j) q -> p j q", j=4))
-        for quad in range(4):
+        key_words = [sb.tile([P, T], U8, name="key_words%d" % h, align_bytes=64) for h in range(2)]
+        nc.sync.dma_start(out=key_words[0][:].bitcast(I32), in_=keys_words[0, :, :T].bitcast(I32))
+        for r in range(4):
             nc.scalar.dma_start(
-                out=key_scales[32 * quad : 32 * quad + 4, :].bitcast(I32),
-                in_=keys_scales[0, 4 * quad : 4 * quad + 4, :].bitcast(I32),
+                out=key_scales[r:P:32, :].bitcast(I32), in_=keys_scales[0, r:16:4, :].bitcast(I32)
             )
-        key_words = sb.tile([P, 2 * T], U8, name="key_words", align_bytes=64)
-        nc.sync.dma_start(out=key_words[:].bitcast(I32), in_=keys_words[0].bitcast(I32))
         q2_raw = sb.tile([P, 4, Q], F32, name="q2_raw")
         nc.sync.dma_start(out=q2_raw[:], in_=query2.rearrange("(p j) q -> p j q", j=4))
+        nc.sync.dma_start(out=key_words[1][:].bitcast(I32), in_=keys_words[0, :, T:].bitcast(I32))
         list1 = lists.tile([P, SLOTS // 16], U16, name="list1")
         list2 = lists.tile([P, SLOTS // 16], U16, name="list2")
         list3 = lists.tile([P, SLOTS // 16], U16, name="list3")
@@ -53,7 +52,6 @@ def tile_attend_quotaratio_lean_twiceput_heads_kernel(
         share_sb = sb.tile([P, 1], F32, name="share_sb")
         old_sb = sb.tile([P, T], F32, name="old_sb")
         nc.sync.dma_start(list1[:], offs)
-        nc.sync.dma_start(out=lam_sb[:], in_=lam)
         nc.sync.dma_start(list2[:], offs2)
         nc.sync.dma_start(list3[:], offs3)
         nc.sync.dma_start(out=old_sb[:], in_=old)
@@ -65,10 +63,11 @@ def tile_attend_quotaratio_lean_twiceput_heads_kernel(
         nc.vector.memset(f1[:], 0.0)
         nc.vector.memset(f2[:], 0.0)
         ident = sb.tile([P, P], F32, name="ident")
+        nc.gpsimd.dma_start(out=lam_sb[:], in_=lam)
         make_identity(nc, ident[:])
 
         def quantise(raw, name):
-            grouped = sb.tile([P, Q, 4], BF16, name=name + "_bf", align_bytes=64)
+            grouped = sb.tile([P, Q, 4], BF16, name=name + "_bf", tag=name + "_bf", align_bytes=64)
             nc.vector.tensor_copy(out=grouped[:], in_=raw[:].rearrange("p j q -> p q j"))
             codes = sb.tile([P, Q], U32, name=name + "_codes", align_bytes=64)
             scales = sb.tile([P, Q], U8, name=name + "_scales", align_bytes=64)
@@ -83,7 +82,7 @@ def tile_attend_quotaratio_lean_twiceput_heads_kernel(
                 out=bank[:],
                 lhsT=codes[:].bitcast(FP8X4),
                 lhsT_scale=scales[:],
-                rhs=key_words[:, 2 * c0 : 2 * (c0 + width)].bitcast(FP4X4),
+                rhs=key_words[c0 // BANK][:, 2 * (c0 % BANK) : 2 * (c0 % BANK + width)].bitcast(FP4X4),
                 rhs_scale=key_scales[:, c0 : c0 + width],
                 start=True,
                 stop=True,
@@ -94,37 +93,45 @@ def tile_attend_quotaratio_lean_twiceput_heads_kernel(
         qc, qs = quantise(q_raw, "q")
         a_banks = [score(qc, qs, c * W, W, "bank%d" % c) for c in range(4)]
         q2c, q2s = quantise(q2_raw, "q2")
-        b_banks = [score(q2c, q2s, h * BANK, BANK, "bank%d" % (4 + h)) for h in range(2)]
+        b_banks = [score(q2c, q2s, c * W, W, "bank%d" % (4 + c)) for c in range(4)]
 
+        f1_late = sb.tile([P, T], F32, name="f1_late", tag="q2_bf", align_bytes=64)
+        nc.gpsimd.memset(f1_late[:], 0.0)
         EARLY = 128
         lam_wide = sb.tile([P, EARLY], F32, name="lam_wide")
         nc.scalar.activation(out=lam_wide[:], in_=lam_sb[:].to_broadcast([P, EARLY]), func=ACT.Copy)
 
         a_sb = sb.tile([P, T], F32, name="a_sb")
         b_sb = sb.tile([P, T], F32, name="b_sb")
-        for c in range(3):
-            nc.scalar.copy(out=a_sb[:, c * W : (c + 1) * W], in_=a_banks[c][:])
-        nc.vector.tensor_copy(out=a_sb[:, 3 * W :], in_=a_banks[3][:])
-        nc.vector.tensor_copy(out=b_sb[:, :BANK], in_=b_banks[0][:])
+        for c in range(4):
+            if c == 3:
+                nc.vector.tensor_copy(out=a_sb[:, c * W : (c + 1) * W], in_=a_banks[c][:])
+            else:
+                nc.scalar.copy(out=a_sb[:, c * W : (c + 1) * W], in_=a_banks[c][:])
+        for c in range(4):
+            nc.vector.tensor_copy(out=b_sb[:, c * W : (c + 1) * W], in_=b_banks[c][:])
 
         H = SLOTS // 2
-        g1 = [sb.tile([P, H], F32, name="g1_%d" % h) for h in range(2)]
-        diff = [sb.tile([P, 2, H], F32, name="diff%d" % h) for h in range(2)]
+        g1 = [sb.tile([P, H], F32, name="g1_%d" % h, tag="g1_%d" % h) for h in range(2)]
+        g2_late = sb.tile([P, H], F32, name="g2_late")
+        diff = sb.tile([P, 2, H], F32, name="diff")
+        diff3_late = sb.tile([P, H], F32, name="diff3_late")
         ex = sb.tile([P, 2, SLOTS], F32, name="ex")
         den = sb.tile([P, SLOTS], F32, name="den")
-        nc.scalar.activation(out=g1[0][:], in_=a_sb[:].indirect(cols(list1, 0, H)), func=ACT.Copy)
-        nc.scalar.copy(out=b_sb[:, BANK:], in_=b_banks[1][:])
-        nc.scalar.activation(out=g1[1][:], in_=a_sb[:].indirect(cols(list1, H, SLOTS)), func=ACT.Copy)
         for h in range(2):
-            nc.vector.tensor_tensor(
-                out=diff[h][:, 0, :], in0=a_sb[:].indirect(cols(list2, h * H, (h + 1) * H)), in1=g1[h][:],
-                op=ALU.subtract,
-            )
-            nc.vector.tensor_tensor(
-                out=diff[h][:, 1, :], in0=b_sb[:].indirect(cols(list3, h * H, (h + 1) * H)), in1=g1[h][:],
-                op=ALU.subtract,
-            )
-            nc.scalar.activation(out=ex[:, :, h * H : (h + 1) * H], in_=diff[h][:], func=ACT.Exp)
+            nc.scalar.activation(out=g1[h][:], in_=a_sb[:].indirect(cols(list1, h * H, (h + 1) * H)), func=ACT.Copy)
+        nc.scalar.activation(out=g2_late[:], in_=a_sb[:].indirect(cols(list2, H, SLOTS)), func=ACT.Copy)
+        nc.vector.tensor_tensor(out=diff[:, 0, :], in0=a_sb[:].indirect(cols(list2, 0, H)), in1=g1[0][:], op=ALU.subtract)
+        nc.vector.tensor_tensor(out=diff[:, 1, :], in0=b_sb[:].indirect(cols(list3, 0, H)), in1=g1[0][:], op=ALU.subtract)
+        nc.vector.tensor_tensor(
+            out=diff3_late[:], in0=b_sb[:].indirect(cols(list3, H, SLOTS)), in1=g1[1][:], op=ALU.subtract
+        )
+        diff2_late = sb.tile([P, H], F32, name="diff2_late", tag="g1_0")
+        nc.vector.tensor_tensor(out=diff2_late[:], in0=g2_late[:], in1=g1[1][:], op=ALU.subtract)
+        nc.scalar.activation(out=ex[:, :, :EARLY], in_=diff[:, :, :EARLY], func=ACT.Exp)
+        nc.scalar.activation(out=ex[:, :, EARLY:H], in_=diff[:, :, EARLY:], func=ACT.Exp)
+        nc.scalar.activation(out=ex[:, 1, H:], in_=diff3_late[:], func=ACT.Exp)
+        nc.scalar.activation(out=ex[:, 0, H:], in_=diff2_late[:], func=ACT.Exp)
 
         def denominator(s0, s1):
             nc.vector.scalar_tensor_tensor(
@@ -132,13 +139,14 @@ def tile_attend_quotaratio_lean_twiceput_heads_kernel(
             )
 
         denominator(0, EARLY)
+        denominator(EARLY, H)
         inv = sb.tile([P, EARLY], F32, name="inv")
         nc.vector.reciprocal(out=inv[:], in_=den[:, :EARLY])
-        denominator(EARLY, SLOTS)
+        denominator(H, SLOTS)
         nc.vector.tensor_tensor(out=f1[:].indirect(cols(list1, 0, EARLY)), in0=inv[:], in1=lam_wide[:], op=ALU.mult)
         nc.vector.tensor_tensor(out=f2[:].indirect(cols(list4, 0, EARLY)), in0=inv[:], in1=lam_wide[:], op=ALU.mult)
 
-        turn_banks = [psum.tile([P, W], F32, name="turn%d" % c, tag="bank%d" % c) for c in range(4)]
+        turn_banks = [psum.tile([P, W], F32, name="turn%d" % c, tag="bank%d" % (4 + c)) for c in range(4)]
         for c in range(4):
             for j in range(2):
                 c0 = c * W + j * P
@@ -155,19 +163,29 @@ def tile_attend_quotaratio_lean_twiceput_heads_kernel(
         for s0, s1 in pieces:
             nc.scalar.activation(out=root_lam[:, s0:s1], in_=root[:, s0:s1], func=ACT.Copy, scale=lam_sb[:])
         nc.vector.tensor_tensor(
-            out=f1[:].indirect(cols(list1, EARLY, SLOTS)), in0=root[:, EARLY:], in1=root_lam[:, EARLY:], op=ALU.mult
+            out=f1[:].indirect(cols(list1, EARLY, H)), in0=root[:, EARLY:H], in1=root_lam[:, EARLY:H], op=ALU.mult
+        )
+        nc.vector.tensor_tensor(
+            out=f1_late[:].indirect(cols(list1, H, SLOTS)), in0=root[:, H:], in1=root_lam[:, H:], op=ALU.mult
         )
         nc.vector.tensor_tensor(
             out=f2[:].indirect(cols(list4, EARLY, SLOTS)), in0=root[:, EARLY:], in1=root_lam[:, EARLY:], op=ALU.mult
         )
 
         turned = [sb.tile([P, W], F32, name="turned%d" % c) for c in range(4)]
-        back_banks = [psum.tile([P, W], F32, name="back%d" % c, tag="bank%d" % (4 + c)) for c in range(4)]
+        back_banks = [psum.tile([P, W], F32, name="back%d" % c, tag="bank%d" % c) for c in range(4)]
         for c in range(4):
             for j in range(2):
                 c0 = c * W + j * P
                 nc.tensor.matmul(
                     turn_banks[c][:, j * P : (j + 1) * P], lhsT=f1[:, c0 : c0 + P], rhs=ident[:],
+                    is_transpose=True, start=False, stop=False,
+                )
+        for c in range(4):
+            for j in range(2):
+                c0 = c * W + j * P
+                nc.tensor.matmul(
+                    turn_banks[c][:, j * P : (j + 1) * P], lhsT=f1_late[:, c0 : c0 + P], rhs=ident[:],
                     is_transpose=True, start=False, stop=(j == 1),
                 )
             nc.scalar.copy(out=turned[c][:], in_=turn_banks[c][:])

@@ -38,7 +38,7 @@ def tile_attend_quotaratio_lean_twiceput_heads_kernel(
         key_words = [sb.tile([P, T], U8, name="key_words%d" % h, align_bytes=64) for h in range(2)]
         nc.sync.dma_start(out=key_words[0][:].bitcast(I32), in_=keys_words[0, :, :T].bitcast(I32))
         for r in range(4):
-            nc.scalar.dma_start(
+            nc.sync.dma_start(
                 out=key_scales[r:P:32, :].bitcast(I32), in_=keys_scales[0, r:16:4, :].bitcast(I32)
             )
         q2_raw = sb.tile([P, 4, Q], F32, name="q2_raw")
@@ -68,7 +68,10 @@ def tile_attend_quotaratio_lean_twiceput_heads_kernel(
 
         def quantise(raw, name):
             grouped = sb.tile([P, Q, 4], BF16, name=name + "_bf", tag=name + "_bf", align_bytes=64)
-            nc.vector.tensor_copy(out=grouped[:], in_=raw[:].rearrange("p j q -> p q j"))
+            nc.vector.tensor_copy(
+                out=grouped[:].rearrange("p (c i) j -> p c j i", i=4),
+                in_=raw[:].rearrange("p j (c i) -> p c j i", i=4),
+            )
             codes = sb.tile([P, Q], U32, name=name + "_codes", align_bytes=64)
             scales = sb.tile([P, Q], U8, name=name + "_scales", align_bytes=64)
             nc.vector.quantize_mx(

@@ -54,6 +54,7 @@ def tile_attend_quotaratio_lean_twiceput_heads_kernel(
         nc.sync.dma_start(list1[:], offs)
         nc.sync.dma_start(list2[:], offs2)
         nc.sync.dma_start(list3[:], offs3)
+        nc.sync.dma_start(out=lam_sb[:], in_=lam)
         nc.sync.dma_start(out=old_sb[:], in_=old)
         nc.sync.dma_start(list4[:], offs4)
         nc.sync.dma_start(out=share_sb[:], in_=share2)
@@ -61,18 +62,18 @@ def tile_attend_quotaratio_lean_twiceput_heads_kernel(
         f1 = sb.tile([P, T], F32, name="f1")
         f2 = sb.tile([P, T], F32, name="f2")
         nc.vector.memset(f1[:], 0.0)
-        nc.vector.memset(f2[:], 0.0)
+        nc.gpsimd.memset(f2[:], 0.0)
         ident = sb.tile([P, P], F32, name="ident")
-        nc.gpsimd.dma_start(out=lam_sb[:], in_=lam)
         make_identity(nc, ident[:])
 
-        def quantise(raw, name):
+        def quantise(raw, name, on_vector):
             grouped = sb.tile([P, Q, 4], BF16, name=name + "_bf", tag=name + "_bf", align_bytes=64)
-            nc.vector.tensor_copy(
-                out=grouped[:].rearrange("p (c i) j -> p c j i", i=4),
-                in_=raw[:].rearrange("p j (c i) -> p c j i", i=4),
-            )
-            codes = sb.tile([P, Q], U32, name=name + "_codes", align_bytes=64)
+            dst = grouped[:].rearrange("p (c i) j -> p c j i", i=4)
+            src = raw[:].rearrange("p j (c i) -> p c j i", i=4)
+            nc.vector.tensor_copy(out=dst[:, : on_vector // 4], in_=src[:, : on_vector // 4])
+            if on_vector < Q:
+                nc.scalar.copy(out=dst[:, on_vector // 4 :], in_=src[:, on_vector // 4 :])
+            codes = sb.tile([P, Q], U32, name=name + "_codes", tag=name + "_codes", align_bytes=64)
             scales = sb.tile([P, Q], U8, name=name + "_scales", align_bytes=64)
             nc.vector.quantize_mx(
                 out=codes[:].bitcast(FP8X4), scales=scales[:], in_=grouped[:].rearrange("p q j -> p (q j)")
@@ -93,16 +94,16 @@ def tile_attend_quotaratio_lean_twiceput_heads_kernel(
             return bank
 
         W = 256
-        qc, qs = quantise(q_raw, "q")
+        qc, qs = quantise(q_raw, "q", 88)
         a_banks = [score(qc, qs, c * W, W, "bank%d" % c) for c in range(4)]
-        q2c, q2s = quantise(q2_raw, "q2")
+        q2c, q2s = quantise(q2_raw, "q2", Q)
         b_banks = [score(q2c, q2s, c * W, W, "bank%d" % (4 + c)) for c in range(4)]
 
         f1_late = sb.tile([P, T], F32, name="f1_late", tag="q2_bf", align_bytes=64)
         nc.gpsimd.memset(f1_late[:], 0.0)
         EARLY = 128
-        lam_wide = sb.tile([P, EARLY], F32, name="lam_wide")
-        nc.scalar.activation(out=lam_wide[:], in_=lam_sb[:].to_broadcast([P, EARLY]), func=ACT.Copy)
+        lam_wide = sb.tile([P, EARLY], F32, name="lam_wide", tag="q2_codes", align_bytes=64)
+        nc.gpsimd.tensor_copy(out=lam_wide[:], in_=lam_sb[:].to_broadcast([P, EARLY]))
 
         a_sb = sb.tile([P, T], F32, name="a_sb")
         b_sb = sb.tile([P, T], F32, name="b_sb")

from contextlib import ExitStack

import concourse.mybir as mybir
from concourse.masks import make_identity

F32 = mybir.dt.float32
BF16 = mybir.dt.bfloat16
I32 = mybir.dt.int32
U32 = mybir.dt.uint32
U16 = mybir.dt.uint16
U8 = mybir.dt.uint8
FP8X4 = mybir.dt.float8_e4m3fn_x4
FP4X4 = mybir.dt.float4_e2m1fn_x4
ACT = mybir.ActivationFunctionType
ALU = mybir.AluOpType

P = 128
D, T, SLOTS, Q = 512, 1024, 512, 128
BANK = 512
FLOPS = 2 * 2 * D * T * Q


def tile_attend_quotaratio_lean_twiceput_heads_kernel(
    tc, query, query2, keys_words, keys_scales, lam, old, share2, offs, offs2, offs3, offs4, out
):
    nc = tc.nc
    with ExitStack() as ctx:
        lists = ctx.enter_context(tc.tile_pool(name="lists", bufs=1))
        sb = ctx.enter_context(tc.tile_pool(name="sb", bufs=1))
        psum = ctx.enter_context(tc.psum_pool(name="psum", bufs=1))

        def cols(lst, s0, s1):
            return lst[:, s0 // 16 : s1 // 16]

        key_scales = sb.tile([P, T], U8, name="key_scales", align_bytes=64)
        q_raw = sb.tile([P, 4, Q], F32, name="q_raw")
        nc.sync.dma_start(out=q_raw[:], in_=query.rearrange("(p j) q -> p j q", j=4))
        key_words = [sb.tile([P, T], U8, name="key_words%d" % h, align_bytes=64) for h in range(2)]
        nc.sync.dma_start(out=key_words[0][:].bitcast(I32), in_=keys_words[0, :, :T].bitcast(I32))
        for r in range(4):
            nc.sync.dma_start(
                out=key_scales[r:P:32, :].bitcast(I32), in_=keys_scales[0, r:16:4, :].bitcast(I32)
            )
        q2_raw = sb.tile([P, 4, Q], F32, name="q2_raw")
        nc.sync.dma_start(out=q2_raw[:], in_=query2.rearrange("(p j) q -> p j q", j=4))
        nc.sync.dma_start(out=key_words[1][:].bitcast(I32), in_=keys_words[0, :, T:].bitcast(I32))
        list1 = lists.tile([P, SLOTS // 16], U16, name="list1")
        list2 = lists.tile([P, SLOTS // 16], U16, name="list2")
        list3 = lists.tile([P, SLOTS // 16], U16, name="list3")
        list4 = lists.tile([P, SLOTS // 16], U16, name="list4")
        lam_sb = sb.tile([P, 1], F32, name="lam_sb")
        share_sb = sb.tile([P, 1], F32, name="share_sb")
        old_sb = sb.tile([P, T], F32, name="old_sb")
        nc.sync.dma_start(list1[:], offs)
        nc.sync.dma_start(list2[:], offs2)
        nc.sync.dma_start(list3[:], offs3)
        nc.sync.dma_start(out=lam_sb[:], in_=lam)
        nc.sync.dma_start(out=old_sb[:], in_=old)
        nc.sync.dma_start(list4[:], offs4)
        nc.sync.dma_start(out=share_sb[:], in_=share2)

        f1 = sb.tile([P, T], F32, name="f1")
        f2 = sb.tile([P, T], F32, name="f2")
        nc.vector.memset(f1[:], 0.0)
        nc.gpsimd.memset(f2[:], 0.0)
        ident = sb.tile([P, P], F32, name="ident")
        make_identity(nc, ident[:])

        def quantise(raw, name, on_vector):
            grouped = sb.tile([P, Q, 4], BF16, name=name + "_bf", tag=name + "_bf", align_bytes=64)
            dst = grouped[:].rearrange("p (c i) j -> p c j i", i=4)
            src = raw[:].rearrange("p j (c i) -> p c j i", i=4)
            nc.vector.tensor_copy(out=dst[:, : on_vector // 4], in_=src[:, : on_vector // 4])
            if on_vector < Q:
                nc.scalar.copy(out=dst[:, on_vector // 4 :], in_=src[:, on_vector // 4 :])
            codes = sb.tile([P, Q], U32, name=name + "_codes", tag=name + "_codes", align_bytes=64)
            scales = sb.tile([P, Q], U8, name=name + "_scales", align_bytes=64)
            nc.vector.quantize_mx(
                out=codes[:].bitcast(FP8X4), scales=scales[:], in_=grouped[:].rearrange("p q j -> p (q j)")
            )
            return codes, scales

        def score(codes, scales, c0, width, tag):
            bank = psum.tile([P, width], F32, name=tag, tag=tag)
            nc.tensor.matmul_mx(
                out=bank[:],
                lhsT=codes[:].bitcast(FP8X4),
                lhsT_scale=scales[:],
                rhs=key_words[c0 // BANK][:, 2 * (c0 % BANK) : 2 * (c0 % BANK + width)].bitcast(FP4X4),
                rhs_scale=key_scales[:, c0 : c0 + width],
                start=True,
                stop=True,
            )
            return bank

        W = 256
        qc, qs = quantise(q_raw, "q", 88)
        a_banks = [score(qc, qs, c * W, W, "bank%d" % c) for c in range(4)]
        q2c, q2s = quantise(q2_raw, "q2", Q)
        b_banks = [score(q2c, q2s, c * W, W, "bank%d" % (4 + c)) for c in range(4)]

        f1_late = sb.tile([P, T], F32, name="f1_late", tag="q2_bf", align_bytes=64)
        nc.gpsimd.memset(f1_late[:], 0.0)
        EARLY = 128
        lam_wide = sb.tile([P, EARLY], F32, name="lam_wide", tag="q2_codes", align_bytes=64)
        nc.gpsimd.tensor_copy(out=lam_wide[:], in_=lam_sb[:].to_broadcast([P, EARLY]))

        a_sb = sb.tile([P, T], F32, name="a_sb")
        b_sb = sb.tile([P, T], F32, name="b_sb")
        for c in range(4):
            if c == 3:
                nc.vector.tensor_copy(out=a_sb[:, c * W : (c + 1) * W], in_=a_banks[c][:])
            else:
                nc.scalar.copy(out=a_sb[:, c * W : (c + 1) * W], in_=a_banks[c][:])
        for c in range(4):
            nc.vector.tensor_copy(out=b_sb[:, c * W : (c + 1) * W], in_=b_banks[c][:])

        H = SLOTS // 2
        g1 = [sb.tile([P, H], F32, name="g1_%d" % h, tag="g1_%d" % h) for h in range(2)]
        g2_late = sb.tile([P, H], F32, name="g2_late")
        diff = sb.tile([P, 2, H], F32, name="diff")
        diff3_late = sb.tile([P, H], F32, name="diff3_late")
        ex = sb.tile([P, 2, SLOTS], F32, name="ex")
        den = sb.tile([P, SLOTS], F32, name="den")
        for h in range(2):
            nc.scalar.activation(out=g1[h][:], in_=a_sb[:].indirect(cols(list1, h * H, (h + 1) * H)), func=ACT.Copy)
        nc.scalar.activation(out=g2_late[:], in_=a_sb[:].indirect(cols(list2, H, SLOTS)), func=ACT.Copy)
        nc.vector.tensor_tensor(out=diff[:, 0, :], in0=a_sb[:].indirect(cols(list2, 0, H)), in1=g1[0][:], op=ALU.subtract)
        nc.vector.tensor_tensor(out=diff[:, 1, :], in0=b_sb[:].indirect(cols(list3, 0, H)), in1=g1[0][:], op=ALU.subtract)
        nc.vector.tensor_tensor(
            out=diff3_late[:], in0=b_sb[:].indirect(cols(list3, H, SLOTS)), in1=g1[1][:], op=ALU.subtract
        )
        diff2_late = sb.tile([P, H], F32, name="diff2_late", tag="g1_0")
        nc.vector.tensor_tensor(out=diff2_late[:], in0=g2_late[:], in1=g1[1][:], op=ALU.subtract)
        nc.scalar.activation(out=ex[:, :, :EARLY], in_=diff[:, :, :EARLY], func=ACT.Exp)
        nc.scalar.activation(out=ex[:, :, EARLY:H], in_=diff[:, :, EARLY:], func=ACT.Exp)
        nc.scalar.activation(out=ex[:, 1, H:], in_=diff3_late[:], func=ACT.Exp)
        nc.scalar.activation(out=ex[:, 0, H:], in_=diff2_late[:], func=ACT.Exp)

        def denominator(s0, s1):
            nc.vector.scalar_tensor_tensor(
                out=den[:, s0:s1], in0=ex[:, 0, s0:s1], scalar=1.0, in1=ex[:, 1, s0:s1], op0=ALU.add, op1=ALU.add
            )

        denominator(0, EARLY)
        denominator(EARLY, H)
        inv = sb.tile([P, EARLY], F32, name="inv")
        nc.vector.reciprocal(out=inv[:], in_=den[:, :EARLY])
        denominator(H, SLOTS)
        nc.vector.tensor_tensor(out=f1[:].indirect(cols(list1, 0, EARLY)), in0=inv[:], in1=lam_wide[:], op=ALU.mult)
        nc.vector.tensor_tensor(out=f2[:].indirect(cols(list4, 0, EARLY)), in0=inv[:], in1=lam_wide[:], op=ALU.mult)

        turn_banks = [psum.tile([P, W], F32, name="turn%d" % c, tag="bank%d" % (4 + c)) for c in range(4)]
        for c in range(4):
            for j in range(2):
                c0 = c * W + j * P
                nc.tensor.matmul(
                    turn_banks[c][:, j * P : (j + 1) * P], lhsT=old_sb[:, c0 : c0 + P], rhs=ident[:],
                    is_transpose=True, start=(j == 0), stop=False,
                )

        pieces = [(EARLY, H), (H, SLOTS)]
        root = sb.tile([P, SLOTS], F32, name="root")
        root_lam = sb.tile([P, SLOTS], F32, name="root_lam")
        for s0, s1 in pieces:
            nc.scalar.activation(out=root[:, s0:s1], in_=den[:, s0:s1], func=ACT.Abs_reciprocal_sqrt)
        for s0, s1 in pieces:
            nc.scalar.activation(out=root_lam[:, s0:s1], in_=root[:, s0:s1], func=ACT.Copy, scale=lam_sb[:])
        nc.vector.tensor_tensor(
            out=f1[:].indirect(cols(list1, EARLY, H)), in0=root[:, EARLY:H], in1=root_lam[:, EARLY:H], op=ALU.mult
        )
        nc.vector.tensor_tensor(
            out=f1_late[:].indirect(cols(list1, H, SLOTS)), in0=root[:, H:], in1=root_lam[:, H:], op=ALU.mult
        )
        nc.vector.tensor_tensor(
            out=f2[:].indirect(cols(list4, EARLY, SLOTS)), in0=root[:, EARLY:], in1=root_lam[:, EARLY:], op=ALU.mult
        )

        turned = [sb.tile([P, W], F32, name="turned%d" % c) for c in range(4)]
        back_banks = [psum.tile([P, W], F32, name="back%d" % c, tag="bank%d" % c) for c in range(4)]
        for c in range(4):
            for j in range(2):
                c0 = c * W + j * P
                nc.tensor.matmul(
                    turn_banks[c][:, j * P : (j + 1) * P], lhsT=f1[:, c0 : c0 + P], rhs=ident[:],
                    is_transpose=True, start=False, stop=False,
                )
        for c in range(4):
            for j in range(2):
                c0 = c * W + j * P
                nc.tensor.matmul(
                    turn_banks[c][:, j * P : (j + 1) * P], lhsT=f1_late[:, c0 : c0 + P], rhs=ident[:],
                    is_transpose=True, start=False, stop=(j == 1),
                )
            nc.scalar.copy(out=turned[c][:], in_=turn_banks[c][:])
        for c in range(4):
            for j in range(2):
                nc.tensor.transpose(back_banks[c][:, j * P : (j + 1) * P], turned[c][:, j * P : (j + 1) * P], ident[:])

        for c in range(T // W):
            res = sb.tile([P, W], F32, name="res%d" % c)
            nc.vector.scalar_tensor_tensor(
                out=res[:], in0=f2[:, c * W : (c + 1) * W], scalar=share_sb[:], in1=back_banks[c][:],
                op0=ALU.mult, op1=ALU.add,
            )
            nc.sync.dma_start(out=out[:, c * W : (c + 1) * W], in_=res[:])
